import numpy as np
import ml_dtypes


def mxq(x, axis, fmt="e4m3"):
    dtype, down = {"e4m3": (ml_dtypes.float8_e4m3fn, 7), "e5m2": (ml_dtypes.float8_e5m2, 14)}[fmt]
    v = np.moveaxis(np.asarray(x, np.float32).astype(ml_dtypes.bfloat16).astype(np.float64), axis, -1)
    blocks = v.reshape(v.shape[:-1] + (-1, 32))
    amax = np.abs(blocks).max(-1, keepdims=True)
    byte = np.maximum(np.where(amax > 0, np.frexp(amax)[1] - 1 + 127, 0) - down, 1)
    scale = np.exp2(byte - 127.0)
    codes = (blocks / scale).astype(np.float32).astype(dtype).astype(np.float64)
    return np.moveaxis((codes * scale).reshape(v.shape), -1, axis)


WIDE = False


def mx_kscale(k):
    if not WIDE:
        return np.ones(k)
    levels = np.array([10, -10, 5, -5, 0])
    if k % 512:
        return np.exp2(np.random.permutation(np.resize(levels, k // 32))).repeat(32)
    a = np.empty((k // 512, 16))
    for p in range(k // 512):
        a[p, :8] = np.random.permutation(np.resize(levels, 8))
        for g in range(8):
            far = levels[np.abs(levels - a[p, g]) >= 10]
            a[p, g + 8] = far[np.random.randint(len(far))]
    return np.exp2(a.ravel()).repeat(32)


def f64(x):
    return np.asarray(x).astype(np.float64)


def striped(idx):
    return np.tile(idx.reshape(-1, 16).T, (8, 1)).astype(np.uint16)


def unstriped(offs):
    return offs[:16].T.reshape(-1).astype(np.int64)


E2M1 = np.array([0.0, 0.5, 1.0, 1.5, 2.0, 3.0, 4.0, 6.0, -0.0, -0.5, -1.0, -1.5, -2.0, -3.0, -4.0, -6.0])


def pack_weight(w, fmt):
    k, n = w.shape
    w = f64(np.asarray(w, np.float32).astype(ml_dtypes.bfloat16)).reshape(k // 32, 32, n)
    amax = np.abs(w).max(1)
    if fmt == "e4m3":
        byte = np.frexp(amax)[1] - 1 + 127 - 7
    else:
        mant, ex = np.frexp(amax / 6.0)
        byte = np.where(mant > 0.5, ex, ex - 1) + 127
    byte = np.clip(np.where(amax > 0, byte, 1), 1, 254)
    scaled = (w * np.exp2(127.0 - byte)[:, None, :]).reshape(k, n).astype(np.float32)
    by_word = np.ascontiguousarray(scaled.reshape(k // 512, 128, 4, n).transpose(0, 1, 3, 2))
    if fmt == "e4m3":
        words = by_word.astype(ml_dtypes.float8_e4m3fn).view(np.uint8)
    else:
        c = by_word.astype(ml_dtypes.float4_e2m1fn).view(np.uint8) & 0xF
        words = (c[..., 0::2] | (c[..., 1::2] << 4)).reshape(k // 512, 128, 2 * n)
    return np.ascontiguousarray(words), np.ascontiguousarray(byte.astype(np.uint8).reshape(k // 512, 16, n))


def unpack_weight(words, scales, fmt):
    g, _, n = scales.shape
    words = np.ascontiguousarray(words).reshape(g, 128, n, -1)
    if fmt == "e4m3":
        vals = words.view(ml_dtypes.float8_e4m3fn).astype(np.float64)
    else:
        nib = np.empty((g, 128, n, 4), np.uint8)
        nib[..., 0::2] = words & 0xF
        nib[..., 1::2] = words >> 4
        vals = E2M1[nib]
    vals = vals * np.repeat(np.exp2(scales.astype(np.float64) - 127.0), 8, axis=1)[..., None]
    return vals.transpose(0, 1, 3, 2).reshape(g * 512, n)


def gelu(v):
    return 0.5 * v * (1.0 + np.tanh(np.sqrt(2.0 / np.pi) * (v + 0.044715 * v**3)))


K, T, S, H, T2, P, N = 1536, 2048, 1024, 512, 2048, 1024, 768


def setup_inputs():
    n = np.random.standard_normal
    s = mx_kscale(K)[:, None]
    u = mx_kscale(H)[:, None]
    tab_words, tab_scales = pack_weight(n((K, T)) * s, "e4m3")
    w4_words, w4_scales = pack_weight(0.44 / np.sqrt(H) * n((H, N)) / u, "e2m1")
    return {
        "tab_words": tab_words,
        "tab_scales": tab_scales,
        "offs": striped(np.random.permutation(T)[:S]),
        "w1": (0.8 / np.sqrt(K) * n((K, H)) / s * u.T).astype(np.float32),
        "page0": (n((H, T2)) * u).astype(np.float32),
        "hours": (2.5 * n((H, S))).astype(np.float32),
        "offs2": striped(np.random.permutation(T2)[:S]),
        "offs3": striped(np.random.permutation(T2)[:P]),
        "w4_words": w4_words,
        "w4_scales": w4_scales,
        "phase": np.random.uniform(-0.6, 0.6, N).astype(np.float32),
    }


def reference(tab_words, tab_scales, offs, w1, page0, hours, offs2, offs3, w4_words, w4_scales, phase):
    v = unpack_weight(tab_words, tab_scales, "e4m3")[:, unstriped(offs)]
    h = mxq(f64(w1), 0, "e4m3").T @ v
    page = f64(page0).copy()
    l2 = unstriped(offs2)
    keep = 1.0 / (1.0 + np.exp(-f64(hours)))
    page[:, l2] = page[:, l2] * keep + h
    x = page[:, unstriped(offs3)]
    w4 = unpack_weight(w4_words, w4_scales, "e2m1")
    y = w4.T @ mxq(x, 0, "e4m3")
    return np.sin(y + f64(phase)[:, None])

@@ -1,0 +1,207 @@
+import math
+from contextlib import ExitStack
+
+import concourse.mybir as mybir
+
+K, T, S, H, T2, PICKS, N = 1536, 2048, 1024, 512, 2048, 1024, 768
+FLOPS = 2 * K * H * S + 2 * H * N * PICKS
+
+F32 = mybir.dt.float32
+BF16 = mybir.dt.bfloat16
+I32 = mybir.dt.int32
+U32 = mybir.dt.uint32
+U16 = mybir.dt.uint16
+U8 = mybir.dt.uint8
+FP8X4 = mybir.dt.float8_e4m3fn_x4
+FP4X4 = mybir.dt.float4_e2m1fn_x4
+ACT = mybir.ActivationFunctionType
+ALU = mybir.AluOpType
+
+P = 128
+PACK = 4
+K_PASS = P * PACK
+PASSES = K // K_PASS
+BANK = 512
+N_TILES = N // P
+GROUP = 16
+CHUNKS = (128, 256, 256, 256, 128)
+HALF_TILES = N_TILES // 2
+
+
+def tile_list_pump_wear_ageing_kernel(
+    tc, tab_words, tab_scales, offs, w1, page0, hours, offs2, offs3, w4_words, w4_scales, phase, out
+):
+    nc = tc.nc
+    with ExitStack() as ctx:
+        lists = ctx.enter_context(tc.tile_pool(name="lists", bufs=1))
+        held = ctx.enter_context(tc.tile_pool(name="held", bufs=1))
+        ring = ctx.enter_context(tc.tile_pool(name="ring", bufs=3))
+        psum = ctx.enter_context(tc.psum_pool(name="psum", bufs=8))
+
+        pick = lists.tile([P, S // GROUP], U16, name="pick")
+        place = lists.tile([P, S // GROUP], U16, name="place")
+        read = lists.tile([P, PICKS // GROUP], U16, name="read")
+
+        tab_sc = held.tile([P, T], U8, name="tab_sc", align_bytes=64)
+        w4_sc = held.tile([P, N], U8, name="w4_sc", align_bytes=64)
+        nc.vector.memset(tab_sc[:].bitcast(I32), 0)
+        nc.vector.memset(w4_sc[:].bitcast(I32), 0)
+
+        nc.sync.dma_start(pick[:], offs)
+        for q in range(4):
+            nc.scalar.dma_start(
+                out=tab_sc[32 * q : 32 * q + 4 * PASSES, :].bitcast(I32),
+                in_=tab_scales[:, 4 * q : 4 * q + 4, :].bitcast(I32),
+            )
+
+        w1_raw, tab_w = [], []
+        for a in range(PASSES):
+            raw = held.tile([P, PACK, H], F32, name=f"w1_raw{a}")
+            nc.sync.dma_start(
+                out=raw[:], in_=w1[a * K_PASS : (a + 1) * K_PASS, :].rearrange("(p j) c -> p j c", j=PACK)
+            )
+            words = held.tile([P, T], I32, name=f"tab_w{a}")
+            nc.sync.dma_start(out=words[:], in_=tab_words[a].rearrange("p t i -> p (t i)").bitcast(I32))
+            w1_raw.append(raw)
+            tab_w.append(words)
+
+        nc.sync.dma_start(place[:], offs2)
+        page_rows = page0.rearrange("(p t) c -> t p c", t=PACK)
+        hour_rows = hours.rearrange("(p t) c -> t p c", t=PACK)
+        pages, keeps = [], []
+        for t in range(PACK):
+            keep = held.tile([P, S], F32, name=f"keep{t}")
+            nc.sync.dma_start(out=keep[:], in_=hour_rows[t])
+            page = held.tile([P, T2], F32, name=f"page{t}")
+            nc.sync.dma_start(out=page[:], in_=page_rows[t])
+            pages.append(page)
+            keeps.append(keep)
+
+        nc.sync.dma_start(read[:], offs3)
+        w4_w = held.tile([P, 2 * N], U8, name="w4_w", align_bytes=64)
+        nc.sync.dma_start(out=w4_w[:].bitcast(I32), in_=w4_words[0].bitcast(I32))
+        for q in range(4):
+            nc.sync.dma_start(
+                out=w4_sc[32 * q : 32 * q + 4, :].bitcast(I32),
+                in_=w4_scales[0, 4 * q : 4 * q + 4, :].bitcast(I32),
+            )
+        phase_sb = held.tile([P, N_TILES], F32, name="phase_sb")
+        with nc.allow_non_contiguous_dma(reason="one phase value for each output row"):
+            nc.sync.dma_start(out=phase_sb[:], in_=phase.rearrange("(c p) -> p c", p=P))
+
+        got_sc = held.tile([P, S], U8, name="got_sc", align_bytes=64)
+        nc.vector.tensor_copy(got_sc[:], tab_sc[:].indirect(pick[:]))
+
+        h_banks = [
+            [psum.tile([P, BANK], F32, name=f"h_bank{t}_{b}", tag="bank") for b in range(S // BANK)]
+            for t in range(PACK)
+        ]
+        for a in range(PASSES):
+            grouped = held.tile([P, PACK * H], BF16, name=f"w1_grouped{a}", align_bytes=64)
+            nc.scalar.copy(
+                out=grouped[:].rearrange("p (t m j) -> p m j t", t=PACK, j=PACK),
+                in_=w1_raw[a][:].rearrange("p j (m t) -> p m j t", t=PACK),
+            )
+            w1_codes = held.tile([P, H], U32, name=f"w1_codes{a}", align_bytes=64)
+            w1_sc = held.tile([P, H], U8, name=f"w1_sc{a}", align_bytes=64)
+            nc.vector.quantize_mx(out=w1_codes[:].bitcast(FP8X4), scales=w1_sc[:], in_=grouped[:])
+            got_w = held.tile([P, S], U32, name=f"got_w{a}", align_bytes=64)
+            nc.vector.tensor_copy(got_w[:], tab_w[a][:].bitcast(U32).indirect(pick[:]))
+            for t in range(PACK):
+                rows = slice(t * P, (t + 1) * P)
+                for b in range(S // BANK):
+                    cols = slice(b * BANK, (b + 1) * BANK)
+                    nc.tensor.matmul_mx(
+                        out=h_banks[t][b][:],
+                        lhsT=w1_codes[:, rows].bitcast(FP8X4),
+                        lhsT_scale=w1_sc[:, rows],
+                        rhs=got_w[:, cols].bitcast(FP8X4),
+                        rhs_scale=got_sc[4 * a : P, cols],
+                        start=(a == 0),
+                        stop=(a == PASSES - 1),
+                    )
+
+        for t in range(PACK):
+            nc.scalar.activation(out=keeps[t][:], in_=keeps[t][:], func=ACT.Sigmoid)
+            h = held.tile([P, S], F32, name=f"h{t}")
+            for b in range(S // BANK):
+                nc.scalar.copy(out=h[:, b * BANK : (b + 1) * BANK], in_=h_banks[t][b][:])
+            aged = held.tile([P, S], F32, name=f"aged{t}", tag=f"aged{t}")
+            nc.vector.tensor_tensor(aged[:], pages[t][:].indirect(place[:]), keeps[t][:], ALU.mult)
+            nc.vector.tensor_tensor(pages[t][:].indirect(place[:]), aged[:], h[:], ALU.add)
+
+        turns0 = held.tile([P, N_TILES], F32, name="turns0")
+        nc.vector.tensor_scalar_mul(turns0[:], phase_sb[:], 1.0 / (2.0 * math.pi))
+
+        out_rows = out.rearrange("(c p) m -> p c m", p=P)
+        planes_tags = ("planes0", "planes1", f"aged{PACK - 1}", "planes0", "planes1")
+        starts = [sum(CHUNKS[:c]) for c in range(len(CHUNKS))]
+
+        def gather(c):
+            m0, width = starts[c], CHUNKS[c]
+            planes = held.tile([P, PACK, width], BF16, name=f"planes_c{c}", tag=planes_tags[c])
+            for t in range(PACK):
+                nc.vector.tensor_copy(
+                    planes[:, t, :], pages[t][:].indirect(read[:, m0 // GROUP : (m0 + width) // GROUP])
+                )
+            return planes
+
+        def multiply(c, planes):
+            width = CHUNKS[c]
+            x = ring.tile([P, PACK * width], BF16, name="x", align_bytes=64)
+            nc.scalar.copy(
+                out=x[:].rearrange("p (m i t) -> p m t i", i=4, t=PACK),
+                in_=planes[:].rearrange("p t (m i) -> p m t i", i=4),
+            )
+            x_codes = ring.tile([P, width], U32, name="x_codes", align_bytes=64)
+            x_sc = ring.tile([P, width], U8, name="x_sc", align_bytes=64)
+            nc.vector.quantize_mx(out=x_codes[:].bitcast(FP8X4), scales=x_sc[:], in_=x[:])
+            per_bank = BANK // width
+            turns = ring.tile([P, N_TILES, width], F32, name="turns")
+            for n0 in range(0, N_TILES, per_bank):
+                bank = psum.tile([P, BANK], F32, name="y_bank", tag="bank")
+                tiles = range(n0, min(n0 + per_bank, N_TILES))
+                for n in tiles:
+                    nc.tensor.matmul_mx(
+                        out=bank[:, (n - n0) * width : (n - n0 + 1) * width],
+                        lhsT=w4_w[:, 2 * P * n : 2 * P * (n + 1)].bitcast(FP4X4),
+                        lhsT_scale=w4_sc[:, P * n : P * (n + 1)],
+                        rhs=x_codes[:].bitcast(FP8X4),
+                        rhs_scale=x_sc[:],
+                        start=True,
+                        stop=True,
+                    )
+                for n in tiles:
+                    nc.scalar.activation(
+                        out=turns[:, n, :],
+                        in_=bank[:, (n - n0) * width : (n - n0 + 1) * width],
+                        func=ACT.Identity,
+                        bias=turns0[:, n : n + 1],
+                        scale=1.0 / (2.0 * math.pi),
+                    )
+            return turns
+
+        def sine(c, turns):
+            m0, width = starts[c], CHUNKS[c]
+            halves = [slice(0, HALF_TILES), slice(HALF_TILES, N_TILES)]
+            whole = ring.tile([P, N_TILES, width], I32, name="whole", bufs=2)
+            result = ring.tile([P, N_TILES, width], F32, name="result", bufs=2)
+            for half in halves:
+                nc.vector.tensor_copy(whole[:, half, :], turns[:, half, :])
+            for half in halves:
+                nc.vector.tensor_tensor(turns[:, half, :], turns[:, half, :], whole[:, half, :], ALU.subtract)
+            for half in halves:
+                nc.scalar.activation(
+                    out=result[:, half, :], in_=turns[:, half, :], func=ACT.Sin, scale=2.0 * math.pi
+                )
+                nc.sync.dma_start(out=out_rows[:, half, m0 : m0 + width], in_=result[:, half, :])
+
+        planes = {0: gather(0), 1: gather(1)}
+        turns = {}
+        for c in range(len(CHUNKS)):
+            turns[c] = multiply(c, planes[c])
+            if c + 2 < len(CHUNKS):
+                planes[c + 2] = gather(c + 2)
+            if c >= 1:
+                sine(c - 1, turns[c - 1])
+        sine(len(CHUNKS) - 1, turns[len(CHUNKS) - 1])

@@ -48,36 +48,46 @@ def tile_list_pump_wear_ageing_kernel(
         nc.vector.memset(w4_sc[:].bitcast(I32), 0)
 
         nc.sync.dma_start(pick[:], offs)
-        for q in range(4):
-            nc.scalar.dma_start(
-                out=tab_sc[32 * q : 32 * q + 4 * PASSES, :].bitcast(I32),
-                in_=tab_scales[:, 4 * q : 4 * q + 4, :].bitcast(I32),
-            )
-
+        sc_rows = held.tile([P, T // 4], I32, name="sc_rows")
         w1_raw, tab_w = [], []
-        for a in range(PASSES):
+
+        def load_w1(a):
             raw = held.tile([P, PACK, H], F32, name=f"w1_raw{a}")
             nc.sync.dma_start(
                 out=raw[:], in_=w1[a * K_PASS : (a + 1) * K_PASS, :].rearrange("(p j) c -> p j c", j=PACK)
             )
+            w1_raw.append(raw)
+
+        def load_table(a):
             words = held.tile([P, T], I32, name=f"tab_w{a}")
             nc.sync.dma_start(out=words[:], in_=tab_words[a].rearrange("p t i -> p (t i)").bitcast(I32))
-            w1_raw.append(raw)
             tab_w.append(words)
 
-        nc.sync.dma_start(place[:], offs2)
+        load_table(0)
+        load_w1(0)
+        for q in range(4):
+            live = slice(32 * q, 32 * q + 4 * PASSES)
+            nc.sync.dma_start(out=sc_rows[live, :], in_=tab_scales[:, 4 * q : 4 * q + 4, :].bitcast(I32))
         page_rows = page0.rearrange("(p t) c -> t p c", t=PACK)
         hour_rows = hours.rearrange("(p t) c -> t p c", t=PACK)
-        pages, keeps = [], []
-        for t in range(PACK):
-            keep = held.tile([P, S], F32, name=f"keep{t}")
-            nc.sync.dma_start(out=keep[:], in_=hour_rows[t])
-            page = held.tile([P, T2], F32, name=f"page{t}")
-            nc.sync.dma_start(out=page[:], in_=page_rows[t])
-            pages.append(page)
-            keeps.append(keep)
+        keeps = [held.tile([P, S], F32, name=f"keep{t}", tag=f"keep{t}") for t in range(PACK)]
+        pages = [held.tile([P, T2], F32, name=f"page{t}") for t in range(PACK)]
+        nc.sync.dma_start(out=keeps[0][:], in_=hour_rows[0])
+        for a in range(1, PASSES):
+            load_w1(a)
+            load_table(a)
 
-        nc.sync.dma_start(read[:], offs3)
+        nc.sync.dma_start(place[:], offs2)
+        for t in range(PACK):
+            if t > 0:
+                nc.sync.dma_start(out=keeps[t][:], in_=hour_rows[t])
+            nc.sync.dma_start(out=pages[t][:], in_=page_rows[t])
+            if t == 1:
+                nc.sync.dma_start(read[:], offs3)
+                phase_sb = held.tile([P, N_TILES], F32, name="phase_sb")
+                with nc.allow_non_contiguous_dma(reason="one phase value for each output row"):
+                    nc.sync.dma_start(out=phase_sb[:], in_=phase.rearrange("(c p) -> p c", p=P))
+
         w4_w = held.tile([P, 2 * N], U8, name="w4_w", align_bytes=64)
         nc.sync.dma_start(out=w4_w[:].bitcast(I32), in_=w4_words[0].bitcast(I32))
         for q in range(4):
@@ -85,11 +95,13 @@ def tile_list_pump_wear_ageing_kernel(
                 out=w4_sc[32 * q : 32 * q + 4, :].bitcast(I32),
                 in_=w4_scales[0, 4 * q : 4 * q + 4, :].bitcast(I32),
             )
-        phase_sb = held.tile([P, N_TILES], F32, name="phase_sb")
-        with nc.allow_non_contiguous_dma(reason="one phase value for each output row"):
-            nc.sync.dma_start(out=phase_sb[:], in_=phase.rearrange("(c p) -> p c", p=P))
 
         got_sc = held.tile([P, S], U8, name="got_sc", align_bytes=64)
+        got_ws = [held.tile([P, S], U32, name=f"got_w{a}", align_bytes=64) for a in range(PASSES)]
+        nc.vector.tensor_copy(got_ws[0][:], tab_w[0][:].bitcast(U32).indirect(pick[:]))
+        for q in range(4):
+            live = slice(32 * q, 32 * q + 4 * PASSES)
+            nc.vector.tensor_copy(tab_sc[live, :].bitcast(I32), sc_rows[live, :])
         nc.vector.tensor_copy(got_sc[:], tab_sc[:].indirect(pick[:]))
 
         h_banks = [
@@ -97,6 +109,8 @@ def tile_list_pump_wear_ageing_kernel(
             for t in range(PACK)
         ]
         for a in range(PASSES):
+            if a == 1:
+                nc.scalar.activation(out=keeps[0][:], in_=keeps[0][:], func=ACT.Sigmoid)
             grouped = held.tile([P, PACK * H], BF16, name=f"w1_grouped{a}", align_bytes=64)
             nc.scalar.copy(
                 out=grouped[:].rearrange("p (t m j) -> p m j t", t=PACK, j=PACK),
@@ -105,8 +119,9 @@ def tile_list_pump_wear_ageing_kernel(
             w1_codes = held.tile([P, H], U32, name=f"w1_codes{a}", align_bytes=64)
             w1_sc = held.tile([P, H], U8, name=f"w1_sc{a}", align_bytes=64)
             nc.vector.quantize_mx(out=w1_codes[:].bitcast(FP8X4), scales=w1_sc[:], in_=grouped[:])
-            got_w = held.tile([P, S], U32, name=f"got_w{a}", align_bytes=64)
-            nc.vector.tensor_copy(got_w[:], tab_w[a][:].bitcast(U32).indirect(pick[:]))
+            got_w = got_ws[a]
+            if a > 0:
+                nc.vector.tensor_copy(got_w[:], tab_w[a][:].bitcast(U32).indirect(pick[:]))
             for t in range(PACK):
                 rows = slice(t * P, (t + 1) * P)
                 for b in range(S // BANK):
@@ -121,14 +136,33 @@ def tile_list_pump_wear_ageing_kernel(
                         stop=(a == PASSES - 1),
                     )
 
-        for t in range(PACK):
-            nc.scalar.activation(out=keeps[t][:], in_=keeps[t][:], func=ACT.Sigmoid)
-            h = held.tile([P, S], F32, name=f"h{t}")
-            for b in range(S // BANK):
-                nc.scalar.copy(out=h[:, b * BANK : (b + 1) * BANK], in_=h_banks[t][b][:])
+        def fade(t):
+            if t > 0:
+                nc.scalar.activation(out=keeps[t][:], in_=keeps[t][:], func=ACT.Sigmoid)
             aged = held.tile([P, S], F32, name=f"aged{t}", tag=f"aged{t}")
             nc.vector.tensor_tensor(aged[:], pages[t][:].indirect(place[:]), keeps[t][:], ALU.mult)
+            return aged
+
+        def fetch_h(t, tag):
+            h = held.tile([P, S], F32, name=f"h{t}", tag=tag)
+            for b in range(S // BANK):
+                nc.scalar.copy(out=h[:, b * BANK : (b + 1) * BANK], in_=h_banks[t][b][:])
+            return h
+
+        def put(t, aged, h):
             nc.vector.tensor_tensor(pages[t][:].indirect(place[:]), aged[:], h[:], ALU.add)
+
+        hs = {0: fetch_h(0, "h0")}
+        ageds = {0: fade(0)}
+        put(0, ageds[0], hs[0])
+        ageds[1] = fade(1)
+        hs[3] = fetch_h(3, "h3")
+        ageds[2] = fade(2)
+        hs[1] = fetch_h(1, "keep2")
+        ageds[3] = fade(3)
+        hs[2] = fetch_h(2, "keep3")
+        for t in range(1, PACK):
+            put(t, ageds[t], hs[t])
 
         turns0 = held.tile([P, N_TILES], F32, name="turns0")
         nc.vector.tensor_scalar_mul(turns0[:], phase_sb[:], 1.0 / (2.0 * math.pi))

@@ -19,13 +19,23 @@ ALU = mybir.AluOpType
 
 P = 128
 PACK = 4
+QUADS = 4
+QUAD = P // QUADS
+SCALE_ROWS = 4
 K_PASS = P * PACK
 PASSES = K // K_PASS
 BANK = 512
-N_TILES = N // P
 GROUP = 16
-CHUNKS = (128, 256, 256, 256, 128)
-HALF_TILES = N_TILES // 2
+HALF = S // 2
+N_TILES = N // P
+TURN = 2.0 * math.pi
+
+WIDTH = 256
+CHUNKS = PICKS // WIDTH
+PER_BANK = BANK // WIDTH
+RUN = 4
+SCALAR_WEAVES = 2
+SINE_LAG = 2
 
 
 def tile_list_pump_wear_ageing_kernel(
@@ -49,12 +59,13 @@ def tile_list_pump_wear_ageing_kernel(
 
         nc.sync.dma_start(pick[:], offs)
         sc_rows = held.tile([P, T // 4], I32, name="sc_rows")
+        live_rows = [slice(QUAD * q, QUAD * q + SCALE_ROWS * PASSES) for q in range(QUADS)]
         w1_raw, tab_w = [], []
 
         def load_w1(a):
             raw = held.tile([P, PACK, H], F32, name=f"w1_raw{a}")
             nc.sync.dma_start(
-                out=raw[:], in_=w1[a * K_PASS : (a + 1) * K_PASS, :].rearrange("(p j) c -> p j c", j=PACK)
+                out=raw[:], in_=w1[a * K_PASS : (a + 1) * K_PASS, :].rearrange("(p i) r -> p i r", i=PACK)
             )
             w1_raw.append(raw)
 
@@ -65,83 +76,98 @@ def tile_list_pump_wear_ageing_kernel(
 
         load_table(0)
         load_w1(0)
-        for q in range(4):
-            live = slice(32 * q, 32 * q + 4 * PASSES)
-            nc.sync.dma_start(out=sc_rows[live, :], in_=tab_scales[:, 4 * q : 4 * q + 4, :].bitcast(I32))
+        for q in range(QUADS):
+            nc.sync.dma_start(
+                out=sc_rows[live_rows[q], :],
+                in_=tab_scales[:, SCALE_ROWS * q : SCALE_ROWS * (q + 1), :].bitcast(I32),
+            )
         page_rows = page0.rearrange("(p t) c -> t p c", t=PACK)
         hour_rows = hours.rearrange("(p t) c -> t p c", t=PACK)
-        keeps = [held.tile([P, S], F32, name=f"keep{t}", tag=f"keep{t}") for t in range(PACK)]
+        keep_rows = held.tile([P, PACK + 1, S], F32, name="keep_rows")
+        keeps = [keep_rows[:, t, :] for t in range(PACK)]
         pages = [held.tile([P, T2], F32, name=f"page{t}") for t in range(PACK)]
-        nc.sync.dma_start(out=keeps[0][:], in_=hour_rows[0])
+        nc.sync.dma_start(out=keeps[0][:, :HALF], in_=hour_rows[0][:, :HALF])
         for a in range(1, PASSES):
             load_w1(a)
             load_table(a)
 
         nc.sync.dma_start(place[:], offs2)
-        for t in range(PACK):
-            if t > 0:
-                nc.sync.dma_start(out=keeps[t][:], in_=hour_rows[t])
+        nc.sync.dma_start(out=pages[0][:], in_=page_rows[0])
+        late_hours = held.tile([P, HALF], F32, name="late_hours", tag="h0")
+        nc.sync.dma_start(out=late_hours[:], in_=hour_rows[0][:, HALF:])
+
+        def load_slice(t):
+            nc.sync.dma_start(out=keeps[t], in_=hour_rows[t])
             nc.sync.dma_start(out=pages[t][:], in_=page_rows[t])
-            if t == 1:
-                nc.sync.dma_start(read[:], offs3)
-                phase_sb = held.tile([P, N_TILES], F32, name="phase_sb")
-                with nc.allow_non_contiguous_dma(reason="one phase value for each output row"):
-                    nc.sync.dma_start(out=phase_sb[:], in_=phase.rearrange("(c p) -> p c", p=P))
+
+        load_slice(1)
+        nc.sync.dma_start(read[:], offs3)
+        phase_sb = held.tile([P, N_TILES], F32, name="phase_sb")
+        with nc.allow_non_contiguous_dma(reason="one phase value for each output row"):
+            nc.sync.dma_start(out=phase_sb[:], in_=phase.rearrange("(c p) -> p c", p=P))
+        for t in range(2, PACK):
+            load_slice(t)
 
         w4_w = held.tile([P, 2 * N], U8, name="w4_w", align_bytes=64)
         nc.sync.dma_start(out=w4_w[:].bitcast(I32), in_=w4_words[0].bitcast(I32))
-        for q in range(4):
+        for q in range(QUADS):
             nc.sync.dma_start(
-                out=w4_sc[32 * q : 32 * q + 4, :].bitcast(I32),
-                in_=w4_scales[0, 4 * q : 4 * q + 4, :].bitcast(I32),
+                out=w4_sc[QUAD * q : QUAD * q + SCALE_ROWS, :].bitcast(I32),
+                in_=w4_scales[0, SCALE_ROWS * q : SCALE_ROWS * (q + 1), :].bitcast(I32),
             )
 
         got_sc = held.tile([P, S], U8, name="got_sc", align_bytes=64)
-        got_ws = [held.tile([P, S], U32, name=f"got_w{a}", align_bytes=64) for a in range(PASSES)]
-        nc.vector.tensor_copy(got_ws[0][:], tab_w[0][:].bitcast(U32).indirect(pick[:]))
-        for q in range(4):
-            live = slice(32 * q, 32 * q + 4 * PASSES)
-            nc.vector.tensor_copy(tab_sc[live, :].bitcast(I32), sc_rows[live, :])
-        nc.vector.tensor_copy(got_sc[:], tab_sc[:].indirect(pick[:]))
+        got_w = [held.tile([P, S], U32, name=f"got_w{a}", align_bytes=64) for a in range(PASSES)]
+
+        def gather_words(a):
+            nc.vector.tensor_copy(got_w[a][:], tab_w[a][:].bitcast(U32).indirect(pick[:]))
 
         h_banks = [
             [psum.tile([P, BANK], F32, name=f"h_bank{t}_{b}", tag="bank") for b in range(S // BANK)]
             for t in range(PACK)
         ]
-        for a in range(PASSES):
-            if a == 1:
-                nc.scalar.activation(out=keeps[0][:], in_=keeps[0][:], func=ACT.Sigmoid)
-            grouped = held.tile([P, PACK * H], BF16, name=f"w1_grouped{a}", align_bytes=64)
+
+        def quantize_w1(a):
+            woven = held.tile([P, PACK * H], BF16, name=f"w1_woven{a}", align_bytes=64)
             nc.scalar.copy(
-                out=grouped[:].rearrange("p (t m j) -> p m j t", t=PACK, j=PACK),
-                in_=w1_raw[a][:].rearrange("p j (m t) -> p m j t", t=PACK),
+                out=woven[:].rearrange("p (t m i) -> p m i t", t=PACK, i=PACK),
+                in_=w1_raw[a][:].rearrange("p i (m t) -> p m i t", t=PACK),
             )
-            w1_codes = held.tile([P, H], U32, name=f"w1_codes{a}", align_bytes=64)
-            w1_sc = held.tile([P, H], U8, name=f"w1_sc{a}", align_bytes=64)
-            nc.vector.quantize_mx(out=w1_codes[:].bitcast(FP8X4), scales=w1_sc[:], in_=grouped[:])
-            got_w = got_ws[a]
-            if a > 0:
-                nc.vector.tensor_copy(got_w[:], tab_w[a][:].bitcast(U32).indirect(pick[:]))
+            codes = held.tile([P, H], U32, name=f"w1_codes{a}", align_bytes=64)
+            scales = held.tile([P, H], U8, name=f"w1_sc{a}", align_bytes=64)
+            nc.vector.quantize_mx(out=codes[:].bitcast(FP8X4), scales=scales[:], in_=woven[:])
+            return codes, scales
+
+        def first_product_pass(a, codes, scales):
             for t in range(PACK):
                 rows = slice(t * P, (t + 1) * P)
                 for b in range(S // BANK):
                     cols = slice(b * BANK, (b + 1) * BANK)
                     nc.tensor.matmul_mx(
                         out=h_banks[t][b][:],
-                        lhsT=w1_codes[:, rows].bitcast(FP8X4),
-                        lhsT_scale=w1_sc[:, rows],
-                        rhs=got_w[:, cols].bitcast(FP8X4),
-                        rhs_scale=got_sc[4 * a : P, cols],
+                        lhsT=codes[:, rows].bitcast(FP8X4),
+                        lhsT_scale=scales[:, rows],
+                        rhs=got_w[a][:, cols].bitcast(FP8X4),
+                        rhs_scale=got_sc[SCALE_ROWS * a : P, cols],
                         start=(a == 0),
                         stop=(a == PASSES - 1),
                     )
 
-        def fade(t):
-            if t > 0:
-                nc.scalar.activation(out=keeps[t][:], in_=keeps[t][:], func=ACT.Sigmoid)
-            aged = held.tile([P, S], F32, name=f"aged{t}", tag=f"aged{t}")
-            nc.vector.tensor_tensor(aged[:], pages[t][:].indirect(place[:]), keeps[t][:], ALU.mult)
-            return aged
+        gather_words(0)
+        for q in range(QUADS):
+            nc.vector.tensor_copy(tab_sc[live_rows[q], :].bitcast(I32), sc_rows[live_rows[q], :])
+        nc.vector.tensor_copy(got_sc[:], tab_sc[:].indirect(pick[:]))
+        first_product_pass(0, *quantize_w1(0))
+        nc.scalar.activation(out=keeps[0][:, :HALF], in_=keeps[0][:, :HALF], func=ACT.Sigmoid)
+        for a in range(1, PASSES):
+            codes, scales = quantize_w1(a)
+            gather_words(a)
+            first_product_pass(a, codes, scales)
+
+        def fade(aged, t, j0, j1):
+            nc.vector.tensor_tensor(
+                aged[:, j0:j1], pages[t][:].indirect(place[:, j0 // GROUP : j1 // GROUP]), keeps[t][:, j0:j1], ALU.mult
+            )
 
         def fetch_h(t, tag):
             h = held.tile([P, S], F32, name=f"h{t}", tag=tag)
@@ -149,55 +175,55 @@ def tile_list_pump_wear_ageing_kernel(
                 nc.scalar.copy(out=h[:, b * BANK : (b + 1) * BANK], in_=h_banks[t][b][:])
             return h
 
-        def put(t, aged, h):
+        def gather_x(picked, c, t):
+            entries = read[:, c * WIDTH // GROUP : (c + 1) * WIDTH // GROUP]
+            nc.vector.tensor_copy(picked[:, t, :], pages[t][:].indirect(entries))
+
+        even_picked = keep_rows[:, 1:, : WIDTH // 2].bitcast(BF16)
+        h_tags = ("h0", "aged0", "h0", "aged1")
+        for t in range(PACK):
+            aged = held.tile([P, S], F32, name=f"aged{t}", tag=f"aged{t}")
+            if t == 0:
+                nc.scalar.activation(out=keeps[0][:, HALF:], in_=late_hours[:], func=ACT.Sigmoid)
+                fade(aged, 0, 0, HALF)
+                fade(aged, 0, HALF, S)
+            else:
+                nc.scalar.activation(out=keeps[t], in_=keeps[t], func=ACT.Sigmoid)
+                fade(aged, t, 0, S)
+            h = fetch_h(t, h_tags[t])
+            if t > 0:
+                gather_x(even_picked, 0, t - 1)
             nc.vector.tensor_tensor(pages[t][:].indirect(place[:]), aged[:], h[:], ALU.add)
-
-        hs = {0: fetch_h(0, "h0")}
-        ageds = {0: fade(0)}
-        put(0, ageds[0], hs[0])
-        ageds[1] = fade(1)
-        hs[3] = fetch_h(3, "h3")
-        ageds[2] = fade(2)
-        hs[1] = fetch_h(1, "keep2")
-        ageds[3] = fade(3)
-        hs[2] = fetch_h(2, "keep3")
-        for t in range(1, PACK):
-            put(t, ageds[t], hs[t])
-
-        turns0 = held.tile([P, N_TILES], F32, name="turns0")
-        nc.vector.tensor_scalar_mul(turns0[:], phase_sb[:], 1.0 / (2.0 * math.pi))
+        gather_x(even_picked, 0, PACK - 1)
 
         out_rows = out.rearrange("(c p) m -> p c m", p=P)
-        planes_tags = ("planes0", "planes1", f"aged{PACK - 1}", "planes0", "planes1")
-        starts = [sum(CHUNKS[:c]) for c in range(len(CHUNKS))]
 
-        def gather(c):
-            m0, width = starts[c], CHUNKS[c]
-            planes = held.tile([P, PACK, width], BF16, name=f"planes_c{c}", tag=planes_tags[c])
+        def gather_chunk(c):
+            if c % 2 == 0:
+                picked = even_picked
+            else:
+                picked = held.tile([P, PACK, WIDTH], BF16, name=f"picked{c}", tag=f"aged{PACK - 1}")
             for t in range(PACK):
-                nc.vector.tensor_copy(
-                    planes[:, t, :], pages[t][:].indirect(read[:, m0 // GROUP : (m0 + width) // GROUP])
-                )
-            return planes
+                gather_x(picked, c, t)
+            return picked
 
-        def multiply(c, planes):
-            width = CHUNKS[c]
-            x = ring.tile([P, PACK * width], BF16, name="x", align_bytes=64)
-            nc.scalar.copy(
-                out=x[:].rearrange("p (m i t) -> p m t i", i=4, t=PACK),
-                in_=planes[:].rearrange("p t (m i) -> p m t i", i=4),
+        def second_product(c, picked):
+            x = ring.tile([P, PACK * WIDTH], BF16, name="x", align_bytes=64, bufs=CHUNKS)
+            weave = nc.scalar.copy if c < SCALAR_WEAVES else nc.vector.tensor_copy
+            weave(
+                out=x[:].rearrange("p (m i t) -> p m t i", i=RUN, t=PACK),
+                in_=picked[:, :, :].rearrange("p t (m i) -> p m t i", i=RUN),
             )
-            x_codes = ring.tile([P, width], U32, name="x_codes", align_bytes=64)
-            x_sc = ring.tile([P, width], U8, name="x_sc", align_bytes=64)
+            x_codes = ring.tile([P, WIDTH], U32, name="x_codes", align_bytes=64)
+            x_sc = ring.tile([P, WIDTH], U8, name="x_sc", align_bytes=64)
             nc.vector.quantize_mx(out=x_codes[:].bitcast(FP8X4), scales=x_sc[:], in_=x[:])
-            per_bank = BANK // width
-            turns = ring.tile([P, N_TILES, width], F32, name="turns")
-            for n0 in range(0, N_TILES, per_bank):
+            banks = []
+            for n0 in range(0, N_TILES, PER_BANK):
                 bank = psum.tile([P, BANK], F32, name="y_bank", tag="bank")
-                tiles = range(n0, min(n0 + per_bank, N_TILES))
-                for n in tiles:
+                tiles = [(n0 + i, slice(i * WIDTH, (i + 1) * WIDTH)) for i in range(PER_BANK)]
+                for n, cols in tiles:
                     nc.tensor.matmul_mx(
-                        out=bank[:, (n - n0) * width : (n - n0 + 1) * width],
+                        out=bank[:, cols],
                         lhsT=w4_w[:, 2 * P * n : 2 * P * (n + 1)].bitcast(FP4X4),
                         lhsT_scale=w4_sc[:, P * n : P * (n + 1)],
                         rhs=x_codes[:].bitcast(FP8X4),
@@ -205,37 +231,43 @@ def tile_list_pump_wear_ageing_kernel(
                         start=True,
                         stop=True,
                     )
-                for n in tiles:
+                whole = ring.tile([P, BANK], I32, name="whole", bufs=6)
+                if c == CHUNKS - 1:
+                    for n, cols in tiles:
+                        nc.vector.tensor_scalar(
+                            whole[:, cols], bank[:, cols], phase_sb[:, n : n + 1], 1.0 / TURN, ALU.add, ALU.mult
+                        )
+                else:
+                    angle = ring.tile([P, BANK], F32, name="angle", bufs=4)
+                    for n, cols in tiles:
+                        nc.scalar.activation(
+                            out=angle[:, cols], in_=bank[:, cols], func=ACT.Identity, bias=phase_sb[:, n : n + 1]
+                        )
+                    nc.gpsimd.tensor_scalar(whole[:], angle[:], 1.0 / TURN, 0.0, ALU.mult, ALU.add)
+                banks.append((bank, n0, tiles, whole))
+            return banks
+
+        def sine(c, banks):
+            for bank, n0, tiles, whole in banks:
+                part = ring.tile([P, BANK], F32, name="part", bufs=6)
+                nc.vector.scalar_tensor_tensor(part[:], bank[:], 1.0 / TURN, whole[:], ALU.mult, ALU.subtract)
+                result = ring.tile([P, BANK], F32, name="result", bufs=8)
+                for n, cols in tiles:
                     nc.scalar.activation(
-                        out=turns[:, n, :],
-                        in_=bank[:, (n - n0) * width : (n - n0 + 1) * width],
-                        func=ACT.Identity,
-                        bias=turns0[:, n : n + 1],
-                        scale=1.0 / (2.0 * math.pi),
+                        out=result[:, cols], in_=part[:, cols], func=ACT.Sin, bias=phase_sb[:, n : n + 1], scale=TURN
                     )
-            return turns
-
-        def sine(c, turns):
-            m0, width = starts[c], CHUNKS[c]
-            halves = [slice(0, HALF_TILES), slice(HALF_TILES, N_TILES)]
-            whole = ring.tile([P, N_TILES, width], I32, name="whole", bufs=2)
-            result = ring.tile([P, N_TILES, width], F32, name="result", bufs=2)
-            for half in halves:
-                nc.vector.tensor_copy(whole[:, half, :], turns[:, half, :])
-            for half in halves:
-                nc.vector.tensor_tensor(turns[:, half, :], turns[:, half, :], whole[:, half, :], ALU.subtract)
-            for half in halves:
-                nc.scalar.activation(
-                    out=result[:, half, :], in_=turns[:, half, :], func=ACT.Sin, scale=2.0 * math.pi
+                nc.sync.dma_start(
+                    out=out_rows[:, n0 : n0 + PER_BANK, c * WIDTH : (c + 1) * WIDTH],
+                    in_=result[:].rearrange("p (n m) -> p n m", m=WIDTH),
                 )
-                nc.sync.dma_start(out=out_rows[:, half, m0 : m0 + width], in_=result[:, half, :])
 
-        planes = {0: gather(0), 1: gather(1)}
-        turns = {}
-        for c in range(len(CHUNKS)):
-            turns[c] = multiply(c, planes[c])
-            if c + 2 < len(CHUNKS):
-                planes[c + 2] = gather(c + 2)
-            if c >= 1:
-                sine(c - 1, turns[c - 1])
-        sine(len(CHUNKS) - 1, turns[len(CHUNKS) - 1])
+        picked = {0: even_picked, 1: gather_chunk(1)}
+        banks = {}
+        for c in range(CHUNKS):
+            banks[c] = second_product(c, picked[c])
+            if c + 2 < CHUNKS:
+                picked[c + 2] = gather_chunk(c + 2)
+            if c >= SINE_LAG:
+                sine(c - SINE_LAG, banks[c - SINE_LAG])
+        for c in range(CHUNKS - SINE_LAG, CHUNKS):
+            sine(c, banks[c])

@@ -194,6 +194,8 @@ def tile_list_pump_wear_ageing_kernel(
             if t > 0:
                 gather_x(even_picked, 0, t - 1)
             nc.vector.tensor_tensor(pages[t][:].indirect(place[:]), aged[:], h[:], ALU.add)
+        warm = held.tile([P, 1], F32, name="warm")
+        nc.scalar.activation(out=warm[:], in_=keep_rows[:, PACK - 1, S - 1 : S], func=ACT.Sin)
         gather_x(even_picked, 0, PACK - 1)
 
         out_rows = out.rearrange("(c p) m -> p c m", p=P)

import math
from contextlib import ExitStack

import concourse.mybir as mybir

K, T, S, H, T2, PICKS, N = 1536, 2048, 1024, 512, 2048, 1024, 768
FLOPS = 2 * K * H * S + 2 * H * N * PICKS

F32 = mybir.dt.float32
BF16 = mybir.dt.bfloat16
I32 = mybir.dt.int32
U32 = mybir.dt.uint32
U16 = mybir.dt.uint16
U8 = mybir.dt.uint8
FP8X4 = mybir.dt.float8_e4m3fn_x4
FP4X4 = mybir.dt.float4_e2m1fn_x4
ACT = mybir.ActivationFunctionType
ALU = mybir.AluOpType

P = 128
PACK = 4
QUADS = 4
QUAD = P // QUADS
SCALE_ROWS = 4
K_PASS = P * PACK
PASSES = K // K_PASS
BANK = 512
GROUP = 16
HALF = S // 2
N_TILES = N // P
TURN = 2.0 * math.pi

WIDTH = 256
CHUNKS = PICKS // WIDTH
PER_BANK = BANK // WIDTH
RUN = 4
SCALAR_WEAVES = 2
SINE_LAG = 2


def tile_list_pump_wear_ageing_kernel(
    tc, tab_words, tab_scales, offs, w1, page0, hours, offs2, offs3, w4_words, w4_scales, phase, out
):
    nc = tc.nc
    with ExitStack() as ctx:
        lists = ctx.enter_context(tc.tile_pool(name="lists", bufs=1))
        held = ctx.enter_context(tc.tile_pool(name="held", bufs=1))
        ring = ctx.enter_context(tc.tile_pool(name="ring", bufs=3))
        psum = ctx.enter_context(tc.psum_pool(name="psum", bufs=8))

        pick = lists.tile([P, S // GROUP], U16, name="pick")
        place = lists.tile([P, S // GROUP], U16, name="place")
        read = lists.tile([P, PICKS // GROUP], U16, name="read")

        tab_sc = held.tile([P, T], U8, name="tab_sc", align_bytes=64)
        w4_sc = held.tile([P, N], U8, name="w4_sc", align_bytes=64)
        nc.vector.memset(tab_sc[:].bitcast(I32), 0)
        nc.vector.memset(w4_sc[:].bitcast(I32), 0)

        nc.sync.dma_start(pick[:], offs)
        sc_rows = held.tile([P, T // 4], I32, name="sc_rows")
        live_rows = [slice(QUAD * q, QUAD * q + SCALE_ROWS * PASSES) for q in range(QUADS)]
        w1_raw, tab_w = [], []

        def load_w1(a):
            raw = held.tile([P, PACK, H], F32, name=f"w1_raw{a}")
            nc.sync.dma_start(
                out=raw[:], in_=w1[a * K_PASS : (a + 1) * K_PASS, :].rearrange("(p i) r -> p i r", i=PACK)
            )
            w1_raw.append(raw)

        def load_table(a):
            words = held.tile([P, T], I32, name=f"tab_w{a}")
            nc.sync.dma_start(out=words[:], in_=tab_words[a].rearrange("p t i -> p (t i)").bitcast(I32))
            tab_w.append(words)

        load_table(0)
        load_w1(0)
        for q in range(QUADS):
            nc.sync.dma_start(
                out=sc_rows[live_rows[q], :],
                in_=tab_scales[:, SCALE_ROWS * q : SCALE_ROWS * (q + 1), :].bitcast(I32),
            )
        page_rows = page0.rearrange("(p t) c -> t p c", t=PACK)
        hour_rows = hours.rearrange("(p t) c -> t p c", t=PACK)
        keep_rows = held.tile([P, PACK + 1, S], F32, name="keep_rows")
        keeps = [keep_rows[:, t, :] for t in range(PACK)]
        pages = [held.tile([P, T2], F32, name=f"page{t}") for t in range(PACK)]
        nc.sync.dma_start(out=keeps[0][:, :HALF], in_=hour_rows[0][:, :HALF])
        for a in range(1, PASSES):
            load_w1(a)
            load_table(a)

        nc.sync.dma_start(place[:], offs2)
        nc.sync.dma_start(out=pages[0][:], in_=page_rows[0])
        late_hours = held.tile([P, HALF], F32, name="late_hours", tag="h0")
        nc.sync.dma_start(out=late_hours[:], in_=hour_rows[0][:, HALF:])

        def load_slice(t):
            nc.sync.dma_start(out=keeps[t], in_=hour_rows[t])
            nc.sync.dma_start(out=pages[t][:], in_=page_rows[t])

        load_slice(1)
        nc.sync.dma_start(read[:], offs3)
        phase_sb = held.tile([P, N_TILES], F32, name="phase_sb")
        with nc.allow_non_contiguous_dma(reason="one phase value for each output row"):
            nc.sync.dma_start(out=phase_sb[:], in_=phase.rearrange("(c p) -> p c", p=P))
        for t in range(2, PACK):
            load_slice(t)

        w4_w = held.tile([P, 2 * N], U8, name="w4_w", align_bytes=64)
        nc.sync.dma_start(out=w4_w[:].bitcast(I32), in_=w4_words[0].bitcast(I32))
        for q in range(QUADS):
            nc.sync.dma_start(
                out=w4_sc[QUAD * q : QUAD * q + SCALE_ROWS, :].bitcast(I32),
                in_=w4_scales[0, SCALE_ROWS * q : SCALE_ROWS * (q + 1), :].bitcast(I32),
            )

        got_sc = held.tile([P, S], U8, name="got_sc", align_bytes=64)
        got_w = [held.tile([P, S], U32, name=f"got_w{a}", align_bytes=64) for a in range(PASSES)]

        def gather_words(a):
            nc.vector.tensor_copy(got_w[a][:], tab_w[a][:].bitcast(U32).indirect(pick[:]))

        h_banks = [
            [psum.tile([P, BANK], F32, name=f"h_bank{t}_{b}", tag="bank") for b in range(S // BANK)]
            for t in range(PACK)
        ]

        def quantize_w1(a):
            woven = held.tile([P, PACK * H], BF16, name=f"w1_woven{a}", align_bytes=64)
            nc.scalar.copy(
                out=woven[:].rearrange("p (t m i) -> p m i t", t=PACK, i=PACK),
                in_=w1_raw[a][:].rearrange("p i (m t) -> p m i t", t=PACK),
            )
            codes = held.tile([P, H], U32, name=f"w1_codes{a}", align_bytes=64)
            scales = held.tile([P, H], U8, name=f"w1_sc{a}", align_bytes=64)
            nc.vector.quantize_mx(out=codes[:].bitcast(FP8X4), scales=scales[:], in_=woven[:])
            return codes, scales

        def first_product_pass(a, codes, scales):
            for t in range(PACK):
                rows = slice(t * P, (t + 1) * P)
                for b in range(S // BANK):
                    cols = slice(b * BANK, (b + 1) * BANK)
                    nc.tensor.matmul_mx(
                        out=h_banks[t][b][:],
                        lhsT=codes[:, rows].bitcast(FP8X4),
                        lhsT_scale=scales[:, rows],
                        rhs=got_w[a][:, cols].bitcast(FP8X4),
                        rhs_scale=got_sc[SCALE_ROWS * a : P, cols],
                        start=(a == 0),
                        stop=(a == PASSES - 1),
                    )

        gather_words(0)
        for q in range(QUADS):
            nc.vector.tensor_copy(tab_sc[live_rows[q], :].bitcast(I32), sc_rows[live_rows[q], :])
        nc.vector.tensor_copy(got_sc[:], tab_sc[:].indirect(pick[:]))
        first_product_pass(0, *quantize_w1(0))
        nc.scalar.activation(out=keeps[0][:, :HALF], in_=keeps[0][:, :HALF], func=ACT.Sigmoid)
        for a in range(1, PASSES):
            codes, scales = quantize_w1(a)
            gather_words(a)
            first_product_pass(a, codes, scales)

        def fade(aged, t, j0, j1):
            nc.vector.tensor_tensor(
                aged[:, j0:j1], pages[t][:].indirect(place[:, j0 // GROUP : j1 // GROUP]), keeps[t][:, j0:j1], ALU.mult
            )

        def fetch_h(t, tag):
            h = held.tile([P, S], F32, name=f"h{t}", tag=tag)
            for b in range(S // BANK):
                nc.scalar.copy(out=h[:, b * BANK : (b + 1) * BANK], in_=h_banks[t][b][:])
            return h

        def gather_x(picked, c, t):
            entries = read[:, c * WIDTH // GROUP : (c + 1) * WIDTH // GROUP]
            nc.vector.tensor_copy(picked[:, t, :], pages[t][:].indirect(entries))

        even_picked = keep_rows[:, 1:, : WIDTH // 2].bitcast(BF16)
        h_tags = ("h0", "aged0", "h0", "aged1")
        for t in range(PACK):
            aged = held.tile([P, S], F32, name=f"aged{t}", tag=f"aged{t}")
            if t == 0:
                nc.scalar.activation(out=keeps[0][:, HALF:], in_=late_hours[:], func=ACT.Sigmoid)
                fade(aged, 0, 0, HALF)
                fade(aged, 0, HALF, S)
            else:
                nc.scalar.activation(out=keeps[t], in_=keeps[t], func=ACT.Sigmoid)
                fade(aged, t, 0, S)
            h = fetch_h(t, h_tags[t])
            if t > 0:
                gather_x(even_picked, 0, t - 1)
            nc.vector.tensor_tensor(pages[t][:].indirect(place[:]), aged[:], h[:], ALU.add)
        warm = held.tile([P, 1], F32, name="warm")
        nc.scalar.activation(out=warm[:], in_=keep_rows[:, PACK - 1, S - 1 : S], func=ACT.Sin)
        gather_x(even_picked, 0, PACK - 1)

        out_rows = out.rearrange("(c p) m -> p c m", p=P)

        def gather_chunk(c):
            if c % 2 == 0:
                picked = even_picked
            else:
                picked = held.tile([P, PACK, WIDTH], BF16, name=f"picked{c}", tag=f"aged{PACK - 1}")
            for t in range(PACK):
                gather_x(picked, c, t)
            return picked

        def second_product(c, picked):
            x = ring.tile([P, PACK * WIDTH], BF16, name="x", align_bytes=64, bufs=CHUNKS)
            weave = nc.scalar.copy if c < SCALAR_WEAVES else nc.vector.tensor_copy
            weave(
                out=x[:].rearrange("p (m i t) -> p m t i", i=RUN, t=PACK),
                in_=picked[:, :, :].rearrange("p t (m i) -> p m t i", i=RUN),
            )
            x_codes = ring.tile([P, WIDTH], U32, name="x_codes", align_bytes=64)
            x_sc = ring.tile([P, WIDTH], U8, name="x_sc", align_bytes=64)
            nc.vector.quantize_mx(out=x_codes[:].bitcast(FP8X4), scales=x_sc[:], in_=x[:])
            banks = []
            for n0 in range(0, N_TILES, PER_BANK):
                bank = psum.tile([P, BANK], F32, name="y_bank", tag="bank")
                tiles = [(n0 + i, slice(i * WIDTH, (i + 1) * WIDTH)) for i in range(PER_BANK)]
                for n, cols in tiles:
                    nc.tensor.matmul_mx(
                        out=bank[:, cols],
                        lhsT=w4_w[:, 2 * P * n : 2 * P * (n + 1)].bitcast(FP4X4),
                        lhsT_scale=w4_sc[:, P * n : P * (n + 1)],
                        rhs=x_codes[:].bitcast(FP8X4),
                        rhs_scale=x_sc[:],
                        start=True,
                        stop=True,
                    )
                whole = ring.tile([P, BANK], I32, name="whole", bufs=6)
                if c == CHUNKS - 1:
                    for n, cols in tiles:
                        nc.vector.tensor_scalar(
                            whole[:, cols], bank[:, cols], phase_sb[:, n : n + 1], 1.0 / TURN, ALU.add, ALU.mult
                        )
                else:
                    angle = ring.tile([P, BANK], F32, name="angle", bufs=4)
                    for n, cols in tiles:
                        nc.scalar.activation(
                            out=angle[:, cols], in_=bank[:, cols], func=ACT.Identity, bias=phase_sb[:, n : n + 1]
                        )
                    nc.gpsimd.tensor_scalar(whole[:], angle[:], 1.0 / TURN, 0.0, ALU.mult, ALU.add)
                banks.append((bank, n0, tiles, whole))
            return banks

        def sine(c, banks):
            for bank, n0, tiles, whole in banks:
                part = ring.tile([P, BANK], F32, name="part", bufs=6)
                nc.vector.scalar_tensor_tensor(part[:], bank[:], 1.0 / TURN, whole[:], ALU.mult, ALU.subtract)
                result = ring.tile([P, BANK], F32, name="result", bufs=8)
                for n, cols in tiles:
                    nc.scalar.activation(
                        out=result[:, cols], in_=part[:, cols], func=ACT.Sin, bias=phase_sb[:, n : n + 1], scale=TURN
                    )
                nc.sync.dma_start(
                    out=out_rows[:, n0 : n0 + PER_BANK, c * WIDTH : (c + 1) * WIDTH],
                    in_=result[:].rearrange("p (n m) -> p n m", m=WIDTH),
                )

        picked = {0: even_picked, 1: gather_chunk(1)}
        banks = {}
        for c in range(CHUNKS):
            banks[c] = second_product(c, picked[c])
            if c + 2 < CHUNKS:
                picked[c + 2] = gather_chunk(c + 2)
            if c >= SINE_LAG:
                sine(c - SINE_LAG, banks[c - SINE_LAG])
        for c in range(CHUNKS - SINE_LAG, CHUNKS):
            sine(c, banks[c])
